import numpy as np
import ml_dtypes


def mxq(x, axis, fmt="e4m3"):
    dtype, down = {"e4m3": (ml_dtypes.float8_e4m3fn, 7), "e5m2": (ml_dtypes.float8_e5m2, 14)}[fmt]
    v = np.moveaxis(np.asarray(x, np.float32).astype(ml_dtypes.bfloat16).astype(np.float64), axis, -1)
    blocks = v.reshape(v.shape[:-1] + (-1, 32))
    amax = np.abs(blocks).max(-1, keepdims=True)
    byte = np.maximum(np.where(amax > 0, np.frexp(amax)[1] - 1 + 127, 0) - down, 1)
    scale = np.exp2(byte - 127.0)
    codes = (blocks / scale).astype(np.float32).astype(dtype).astype(np.float64)
    return np.moveaxis((codes * scale).reshape(v.shape), -1, axis)


WIDE = False


def mx_kscale(k):
    if not WIDE:
        return np.ones(k)
    levels = np.array([10, -10, 5, -5, 0])
    if k % 512:
        return np.exp2(np.random.permutation(np.resize(levels, k // 32))).repeat(32)
    a = np.empty((k // 512, 16))
    for p in range(k // 512):
        a[p, :8] = np.random.permutation(np.resize(levels, 8))
        for g in range(8):
            far = levels[np.abs(levels - a[p, g]) >= 10]
            a[p, g + 8] = far[np.random.randint(len(far))]
    return np.exp2(a.ravel()).repeat(32)


def f64(x):
    return np.asarray(x).astype(np.float64)


def striped8(idx):
    return np.asarray(idx).reshape(8, -1, 16).transpose(0, 2, 1).reshape(128, -1).astype(np.uint16)


def unstriped8(offs):
    return offs.reshape(8, 16, -1).transpose(0, 2, 1).reshape(8, -1).astype(np.int64)


def pick8(x, idx, run):
    r = np.arange(len(x))
    return x[r[:, None], idx[r % (8 * run) // run]]


E2M1 = np.array([0.0, 0.5, 1.0, 1.5, 2.0, 3.0, 4.0, 6.0, -0.0, -0.5, -1.0, -1.5, -2.0, -3.0, -4.0, -6.0])


def pack_weight(w, fmt):
    k, n = w.shape
    w = f64(np.asarray(w, np.float32).astype(ml_dtypes.bfloat16)).reshape(k // 32, 32, n)
    amax = np.abs(w).max(1)
    if fmt == "e4m3":
        byte = np.frexp(amax)[1] - 1 + 127 - 7
    else:
        mant, ex = np.frexp(amax / 6.0)
        byte = np.where(mant > 0.5, ex, ex - 1) + 127
    byte = np.clip(np.where(amax > 0, byte, 1), 1, 254)
    scaled = (w * np.exp2(127.0 - byte)[:, None, :]).reshape(k, n).astype(np.float32)
    by_word = np.ascontiguousarray(scaled.reshape(k // 512, 128, 4, n).transpose(0, 1, 3, 2))
    if fmt == "e4m3":
        words = by_word.astype(ml_dtypes.float8_e4m3fn).view(np.uint8)
    else:
        c = by_word.astype(ml_dtypes.float4_e2m1fn).view(np.uint8) & 0xF
        words = (c[..., 0::2] | (c[..., 1::2] << 4)).reshape(k // 512, 128, 2 * n)
    return np.ascontiguousarray(words), np.ascontiguousarray(byte.astype(np.uint8).reshape(k // 512, 16, n))


def unpack_weight(words, scales, fmt):
    g, _, n = scales.shape
    words = np.ascontiguousarray(words).reshape(g, 128, n, -1)
    if fmt == "e4m3":
        vals = words.view(ml_dtypes.float8_e4m3fn).astype(np.float64)
    else:
        nib = np.empty((g, 128, n, 4), np.uint8)
        nib[..., 0::2] = words & 0xF
        nib[..., 1::2] = words >> 4
        vals = E2M1[nib]
    vals = vals * np.repeat(np.exp2(scales.astype(np.float64) - 127.0), 8, axis=1)[..., None]
    return vals.transpose(0, 1, 3, 2).reshape(g * 512, n)


def sigmoid(v):
    return 1.0 / (1.0 + np.exp(-v))


def bf(x):
    return np.asarray(x, np.float32).astype(ml_dtypes.bfloat16)


def planes(Y):
    r, m = Y.shape
    b = f64(bf(Y)).reshape(r // 32, 32, m)
    amax = np.abs(b).max(1)
    byte = np.clip(np.where(amax > 0, np.frexp(amax)[1] - 1 + 127 - 7, 1), 1, 254)
    codes = (b * np.exp2(127.0 - byte)[:, None, :]).reshape(r, m).astype(np.float32).astype(ml_dtypes.float8_e4m3fn).view(np.uint8)
    words = codes.reshape(r // 512, 128, 4, m).transpose(0, 1, 3, 2)
    return np.ascontiguousarray(words), np.ascontiguousarray(byte.astype(np.uint8).reshape(r // 512, 16, m))


K, T, J, N = 512, 512, 512, 512


def setup_inputs():
    n = np.random.standard_normal
    idx = np.stack([np.random.randint(0, T, J) for _ in range(8)])
    idx2 = np.stack([np.random.randint(0, T, J) for _ in range(8)])
    fk = mx_kscale(K)
    wvp = pack_weight(n((K, N)) * 1 / np.sqrt(K) * fk[:, None], "e2m1")
    wgp = pack_weight(n((K, N)) * 1 / np.sqrt(K) * fk[:, None], "e4m3")
    return {
        "xt": (n((K, T)) / fk[:, None]).astype(np.float32),
        "wv_words": wvp[0],
        "wv_scales": wvp[1],
        "wg_words": wgp[0],
        "wg_scales": wgp[1],
        "offs": striped8(idx),
        "offs2": striped8(idx2),
    }


def reference(xt, wv_words, wv_scales, wg_words, wg_scales, offs, offs2):
    idx = unstriped8(offs)
    idx2 = unstriped8(offs2)
    wvu = unpack_weight(wv_words, wv_scales, "e2m1")
    wgu = unpack_weight(wg_words, wg_scales, "e4m3")
    xtq = mxq(f64(xt), 0, "e4m3")
    v = wvu.T @ xtq
    g = wgu.T @ xtq
    y = pick8(v, idx, 64) * sigmoid(pick8(g, idx2, 64))
    words, scales = planes(y)
    return y, words, scales

@@ -1,0 +1,191 @@
+from contextlib import ExitStack
+
+import concourse.mybir as mybir
+
+K, T, J, N = 512, 512, 512, 512
+FLOPS = 2 * 2 * K * N * T
+
+F32 = mybir.dt.float32
+BF16 = mybir.dt.bfloat16
+I32 = mybir.dt.int32
+U32 = mybir.dt.uint32
+U16 = mybir.dt.uint16
+U8 = mybir.dt.uint8
+FP8X4 = mybir.dt.float8_e4m3fn_x4
+FP4X4 = mybir.dt.float4_e2m1fn_x4
+SIGMOID = mybir.ActivationFunctionType.Sigmoid
+MULT = mybir.AluOpType.mult
+
+P = 128
+PACK = 4
+QUADS = 4
+TOKEN_CHUNK = 256
+SLOT_CHUNK = 256
+LIST_ROWS = 16
+
+
+def tile_list_head_gate_from_other_token_pl_kernel(
+    tc, xt, wv_words, wv_scales, wg_words, wg_scales, offs, offs2, out_0, out_1, out_2
+):
+    nc = tc.nc
+    with ExitStack() as ctx:
+        lists = ctx.enter_context(tc.tile_pool(name="lists", bufs=1))
+        keep = ctx.enter_context(tc.tile_pool(name="keep", bufs=1))
+        psum = ctx.enter_context(tc.psum_pool(name="psum", bufs=1))
+
+        token_chunks = range(T // TOKEN_CHUNK)
+        slot_chunks = range(J // SLOT_CHUNK)
+
+        wg_scales_raw = keep.tile([P, N], U8, name="wg_scales_raw", align_bytes=64)
+        wv_scales_raw = keep.tile([P, N], U8, name="wv_scales_raw", align_bytes=64)
+        nc.vector.memset(wg_scales_raw[:].bitcast(I32), 0)
+        nc.vector.memset(wv_scales_raw[:].bitcast(I32), 0)
+
+        def load_scale_rows(raw, scales):
+            for q in range(QUADS):
+                nc.sync.dma_start(
+                    out=raw[:].bitcast(I32)[32 * q : 32 * q + 4, :],
+                    in_=scales[0, 4 * q : 4 * q + 4, :].bitcast(I32),
+                )
+
+        x_rows = xt.rearrange("(p j) t -> p j t", j=PACK)
+        x_raw = [keep.tile([P, PACK, TOKEN_CHUNK], F32, name=f"x_raw{c}") for c in token_chunks]
+        wg_raw = keep.tile([P, N], I32, name="wg_raw")
+        wv_raw = keep.tile([P, N // 2], I32, name="wv_raw")
+        value_list = lists.tile([P, J // LIST_ROWS], U16, name="value_list")
+        gate_list = lists.tile([P, J // LIST_ROWS], U16, name="gate_list")
+
+        nc.sync.dma_start(out=x_raw[0][:], in_=x_rows[:, :, 0:TOKEN_CHUNK])
+        load_scale_rows(wg_scales_raw, wg_scales)
+        nc.sync.dma_start(out=wg_raw[:], in_=wg_words[0].rearrange("p n r -> p (n r)").bitcast(I32))
+        nc.sync.dma_start(out=wv_raw[:], in_=wv_words[0].bitcast(I32))
+        nc.sync.dma_start(out=x_raw[1][:], in_=x_rows[:, :, TOKEN_CHUNK:T])
+        load_scale_rows(wv_scales_raw, wv_scales)
+        nc.sync.dma_start(gate_list[:], offs2)
+        nc.sync.dma_start(value_list[:], offs)
+
+        wg_dealt = keep.tile([P, N], U32, name="wg_dealt", align_bytes=64)
+        wv_dealt = keep.tile([P, 2 * N], U8, name="wv_dealt", align_bytes=64)
+        wg_scales_dealt = keep.tile([P, N], U8, name="wg_scales_dealt", align_bytes=64)
+
+        def deal(engine_copy, dealt, raw):
+            engine_copy(
+                out=dealt.rearrange("p (t a i) -> p a t i", t=PACK, i=4),
+                in_=raw.rearrange("p (a i t) -> p a t i", t=PACK, i=4),
+            )
+
+        deal(nc.vector.tensor_copy, wg_scales_dealt[:], wg_scales_raw[:])
+        deal(nc.scalar.copy, wg_dealt[:], wg_raw[:].bitcast(U32))
+        deal(nc.scalar.copy, wv_dealt[:].bitcast(U16), wv_raw[:].bitcast(U16))
+
+        x_codes = keep.tile([P, T], U32, name="x_codes", align_bytes=64)
+        x_scales = keep.tile([P, T], U8, name="x_scales", align_bytes=64)
+        for c in token_chunks:
+            grouped = keep.tile([P, TOKEN_CHUNK * PACK], BF16, name=f"x_grouped{c}", tag=f"x_grouped{c}", align_bytes=64)
+            nc.vector.tensor_copy(
+                out=grouped[:].rearrange("p (a i j) -> p a j i", i=4, j=PACK),
+                in_=x_raw[c][:].rearrange("p j (a i) -> p a j i", i=4),
+            )
+            tokens = slice(c * TOKEN_CHUNK, (c + 1) * TOKEN_CHUNK)
+            nc.vector.quantize_mx(out=x_codes[:, tokens].bitcast(FP8X4), scales=x_scales[:, tokens], in_=grouped[:])
+
+        wv_scales_dealt = keep.tile([P, N], U8, name="wv_scales_dealt", tag="x_grouped1", align_bytes=64)
+        deal(nc.vector.tensor_copy, wv_scales_dealt[:], wv_scales_raw[:])
+
+        g_rows = [keep.tile([P, T], F32, name=f"g_rows{t}") for t in range(PACK)]
+        v_rows = [keep.tile([P, T], F32, name=f"v_rows{t}") for t in range(PACK)]
+
+        def product(out, codes, scales_dealt, t, tokens):
+            nc.tensor.matmul_mx(
+                out=out,
+                lhsT=codes,
+                lhsT_scale=scales_dealt[:, t * P : (t + 1) * P],
+                rhs=x_codes[:, tokens].bitcast(FP8X4),
+                rhs_scale=x_scales[:, tokens],
+                start=True,
+                stop=True,
+            )
+
+        def gate_codes(t):
+            return wg_dealt[:, t * P : (t + 1) * P].bitcast(FP8X4)
+
+        def value_codes(t):
+            return wv_dealt[:, 2 * t * P : 2 * (t + 1) * P].bitcast(FP4X4)
+
+        early = slice(0, TOKEN_CHUNK)
+        late = slice(TOKEN_CHUNK, T)
+        on_scalar = nc.scalar.copy
+        on_vector = nc.vector.tensor_copy
+
+        for pair in range(2):
+            bank = psum.tile([P, 2, TOKEN_CHUNK], F32, name=f"g_early{pair}", tag=f"g_bank{pair}")
+            for u in range(2):
+                product(bank[:, u, :], gate_codes(2 * pair + u), wg_scales_dealt, 2 * pair + u, early)
+            for u in range(2):
+                on_scalar(out=g_rows[2 * pair + u][:, early], in_=bank[:, u, :])
+
+        def late_gate(t, engine_copy):
+            bank = psum.tile([P, TOKEN_CHUNK], F32, name=f"g_late{t}", tag=f"g_bank{(t + 2) % PACK}")
+            product(bank[:], gate_codes(t), wg_scales_dealt, t, late)
+            engine_copy(out=g_rows[t][:, late], in_=bank[:])
+
+        def values(t, engine_copy):
+            bank = psum.tile([P, T], F32, name=f"v_bank{t}")
+            product(bank[:], value_codes(t), wv_scales_dealt, t, slice(0, T))
+            engine_copy(out=v_rows[t][:], in_=bank[:])
+
+        y = [keep.tile([P, PACK, SLOT_CHUNK], F32, name=f"y{c}") for c in slot_chunks]
+        y_scales = keep.tile([P, J], U8, name="y_scales", align_bytes=64)
+        y_rows = out_0.rearrange("(p t) j -> p t j", t=PACK)
+        y_words = out_1[0].rearrange("p j r -> p (j r)").bitcast(I32)
+        list_cols = SLOT_CHUNK // LIST_ROWS
+
+        def look_up(t, c):
+            entries = slice(c * list_cols, (c + 1) * list_cols)
+            gate = keep.tile([P, SLOT_CHUNK], F32, name=f"gate{t}_{c}")
+            nc.scalar.activation(out=gate[:], in_=g_rows[t][:].indirect(gate_list[:, entries]), func=SIGMOID)
+            nc.vector.tensor_tensor(y[c][:, t, :], v_rows[t][:].indirect(value_list[:, entries]), gate[:], MULT)
+
+        def store_rows(c, t0, t1):
+            cols = slice(c * SLOT_CHUNK, (c + 1) * SLOT_CHUNK)
+            nc.sync.dma_start(out=y_rows[:, t0:t1, cols], in_=y[c][:, t0:t1, :])
+
+        def quantise_result(c, engine_copy):
+            cols = slice(c * SLOT_CHUNK, (c + 1) * SLOT_CHUNK)
+            grouped = keep.tile([P, SLOT_CHUNK * PACK], BF16, name=f"y_grouped{c}", align_bytes=64)
+            engine_copy(
+                out=grouped[:].rearrange("p (a i t) -> p a t i", i=4, t=PACK),
+                in_=y[c][:].rearrange("p t (a i) -> p a t i", i=4),
+            )
+            codes = keep.tile([P, SLOT_CHUNK], U32, name=f"y_codes{c}", align_bytes=64)
+            nc.vector.quantize_mx(out=codes[:].bitcast(FP8X4), scales=y_scales[:, cols], in_=grouped[:])
+            nc.sync.dma_start(out=y_words[:, cols], in_=codes[:].bitcast(I32))
+
+        late_gate(0, on_scalar)
+        late_gate(1, on_vector)
+        values(0, on_vector)
+        look_up(0, 0)
+        values(1, on_vector)
+        look_up(1, 0)
+        store_rows(0, 0, 2)
+        late_gate(2, on_scalar)
+        values(2, on_vector)
+        look_up(2, 0)
+        late_gate(3, on_scalar)
+        values(3, on_scalar)
+        look_up(3, 0)
+        store_rows(0, 2, 4)
+        for t in range(PACK):
+            look_up(t, 1)
+            if t % 2 == 1:
+                store_rows(1, t - 1, t + 1)
+        quantise_result(0, on_scalar)
+        quantise_result(1, on_vector)
+
+        scale_words = y_scales[:].bitcast(I32)
+        for q in range(QUADS):
+            queue = nc.scalar if q % 2 == 0 else nc.sync
+            queue.dma_start(
+                out=out_2[0, 4 * q : 4 * q + 4, :].bitcast(I32),
+                in_=scale_words[32 * q : 32 * q + 4, :],
+            )

@@ -34,6 +34,11 @@ def tile_list_head_gate_from_other_token_pl_kernel(
         psum = ctx.enter_context(tc.psum_pool(name="psum", bufs=1))
 
         token_chunks = range(T // TOKEN_CHUNK)
+
+        warm_in = keep.tile([P, 1], F32, name="warm_in")
+        warm_out = keep.tile([P, 1], F32, name="warm_out")
+        nc.gpsimd.memset(warm_in[:], 0.0)
+        nc.scalar.activation(out=warm_out[:], in_=warm_in[:], func=SIGMOID)
         slot_chunks = range(J // SLOT_CHUNK)
 
         wg_scales_raw = keep.tile([P, N], U8, name="wg_scales_raw", align_bytes=64)

from contextlib import ExitStack

import concourse.mybir as mybir

K, T, J, N = 512, 512, 512, 512
FLOPS = 2 * 2 * K * N * T

F32 = mybir.dt.float32
BF16 = mybir.dt.bfloat16
I32 = mybir.dt.int32
U32 = mybir.dt.uint32
U16 = mybir.dt.uint16
U8 = mybir.dt.uint8
FP8X4 = mybir.dt.float8_e4m3fn_x4
FP4X4 = mybir.dt.float4_e2m1fn_x4
SIGMOID = mybir.ActivationFunctionType.Sigmoid
MULT = mybir.AluOpType.mult

P = 128
PACK = 4
QUADS = 4
TOKEN_CHUNK = 256
SLOT_CHUNK = 256
LIST_ROWS = 16


def tile_list_head_gate_from_other_token_pl_kernel(
    tc, xt, wv_words, wv_scales, wg_words, wg_scales, offs, offs2, out_0, out_1, out_2
):
    nc = tc.nc
    with ExitStack() as ctx:
        lists = ctx.enter_context(tc.tile_pool(name="lists", bufs=1))
        keep = ctx.enter_context(tc.tile_pool(name="keep", bufs=1))
        psum = ctx.enter_context(tc.psum_pool(name="psum", bufs=1))

        token_chunks = range(T // TOKEN_CHUNK)

        warm_in = keep.tile([P, 1], F32, name="warm_in")
        warm_out = keep.tile([P, 1], F32, name="warm_out")
        nc.gpsimd.memset(warm_in[:], 0.0)
        nc.scalar.activation(out=warm_out[:], in_=warm_in[:], func=SIGMOID)
        slot_chunks = range(J // SLOT_CHUNK)

        wg_scales_raw = keep.tile([P, N], U8, name="wg_scales_raw", align_bytes=64)
        wv_scales_raw = keep.tile([P, N], U8, name="wv_scales_raw", align_bytes=64)
        nc.vector.memset(wg_scales_raw[:].bitcast(I32), 0)
        nc.vector.memset(wv_scales_raw[:].bitcast(I32), 0)

        def load_scale_rows(raw, scales):
            for q in range(QUADS):
                nc.sync.dma_start(
                    out=raw[:].bitcast(I32)[32 * q : 32 * q + 4, :],
                    in_=scales[0, 4 * q : 4 * q + 4, :].bitcast(I32),
                )

        x_rows = xt.rearrange("(p j) t -> p j t", j=PACK)
        x_raw = [keep.tile([P, PACK, TOKEN_CHUNK], F32, name=f"x_raw{c}") for c in token_chunks]
        wg_raw = keep.tile([P, N], I32, name="wg_raw")
        wv_raw = keep.tile([P, N // 2], I32, name="wv_raw")
        value_list = lists.tile([P, J // LIST_ROWS], U16, name="value_list")
        gate_list = lists.tile([P, J // LIST_ROWS], U16, name="gate_list")

        nc.sync.dma_start(out=x_raw[0][:], in_=x_rows[:, :, 0:TOKEN_CHUNK])
        load_scale_rows(wg_scales_raw, wg_scales)
        nc.sync.dma_start(out=wg_raw[:], in_=wg_words[0].rearrange("p n r -> p (n r)").bitcast(I32))
        nc.sync.dma_start(out=wv_raw[:], in_=wv_words[0].bitcast(I32))
        nc.sync.dma_start(out=x_raw[1][:], in_=x_rows[:, :, TOKEN_CHUNK:T])
        load_scale_rows(wv_scales_raw, wv_scales)
        nc.sync.dma_start(gate_list[:], offs2)
        nc.sync.dma_start(value_list[:], offs)

        wg_dealt = keep.tile([P, N], U32, name="wg_dealt", align_bytes=64)
        wv_dealt = keep.tile([P, 2 * N], U8, name="wv_dealt", align_bytes=64)
        wg_scales_dealt = keep.tile([P, N], U8, name="wg_scales_dealt", align_bytes=64)

        def deal(engine_copy, dealt, raw):
            engine_copy(
                out=dealt.rearrange("p (t a i) -> p a t i", t=PACK, i=4),
                in_=raw.rearrange("p (a i t) -> p a t i", t=PACK, i=4),
            )

        deal(nc.vector.tensor_copy, wg_scales_dealt[:], wg_scales_raw[:])
        deal(nc.scalar.copy, wg_dealt[:], wg_raw[:].bitcast(U32))
        deal(nc.scalar.copy, wv_dealt[:].bitcast(U16), wv_raw[:].bitcast(U16))

        x_codes = keep.tile([P, T], U32, name="x_codes", align_bytes=64)
        x_scales = keep.tile([P, T], U8, name="x_scales", align_bytes=64)
        for c in token_chunks:
            grouped = keep.tile([P, TOKEN_CHUNK * PACK], BF16, name=f"x_grouped{c}", tag=f"x_grouped{c}", align_bytes=64)
            nc.vector.tensor_copy(
                out=grouped[:].rearrange("p (a i j) -> p a j i", i=4, j=PACK),
                in_=x_raw[c][:].rearrange("p j (a i) -> p a j i", i=4),
            )
            tokens = slice(c * TOKEN_CHUNK, (c + 1) * TOKEN_CHUNK)
            nc.vector.quantize_mx(out=x_codes[:, tokens].bitcast(FP8X4), scales=x_scales[:, tokens], in_=grouped[:])

        wv_scales_dealt = keep.tile([P, N], U8, name="wv_scales_dealt", tag="x_grouped1", align_bytes=64)
        deal(nc.vector.tensor_copy, wv_scales_dealt[:], wv_scales_raw[:])

        g_rows = [keep.tile([P, T], F32, name=f"g_rows{t}") for t in range(PACK)]
        v_rows = [keep.tile([P, T], F32, name=f"v_rows{t}") for t in range(PACK)]

        def product(out, codes, scales_dealt, t, tokens):
            nc.tensor.matmul_mx(
                out=out,
                lhsT=codes,
                lhsT_scale=scales_dealt[:, t * P : (t + 1) * P],
                rhs=x_codes[:, tokens].bitcast(FP8X4),
                rhs_scale=x_scales[:, tokens],
                start=True,
                stop=True,
            )

        def gate_codes(t):
            return wg_dealt[:, t * P : (t + 1) * P].bitcast(FP8X4)

        def value_codes(t):
            return wv_dealt[:, 2 * t * P : 2 * (t + 1) * P].bitcast(FP4X4)

        early = slice(0, TOKEN_CHUNK)
        late = slice(TOKEN_CHUNK, T)
        on_scalar = nc.scalar.copy
        on_vector = nc.vector.tensor_copy

        for pair in range(2):
            bank = psum.tile([P, 2, TOKEN_CHUNK], F32, name=f"g_early{pair}", tag=f"g_bank{pair}")
            for u in range(2):
                product(bank[:, u, :], gate_codes(2 * pair + u), wg_scales_dealt, 2 * pair + u, early)
            for u in range(2):
                on_scalar(out=g_rows[2 * pair + u][:, early], in_=bank[:, u, :])

        def late_gate(t, engine_copy):
            bank = psum.tile([P, TOKEN_CHUNK], F32, name=f"g_late{t}", tag=f"g_bank{(t + 2) % PACK}")
            product(bank[:], gate_codes(t), wg_scales_dealt, t, late)
            engine_copy(out=g_rows[t][:, late], in_=bank[:])

        def values(t, engine_copy):
            bank = psum.tile([P, T], F32, name=f"v_bank{t}")
            product(bank[:], value_codes(t), wv_scales_dealt, t, slice(0, T))
            engine_copy(out=v_rows[t][:], in_=bank[:])

        y = [keep.tile([P, PACK, SLOT_CHUNK], F32, name=f"y{c}") for c in slot_chunks]
        y_scales = keep.tile([P, J], U8, name="y_scales", align_bytes=64)
        y_rows = out_0.rearrange("(p t) j -> p t j", t=PACK)
        y_words = out_1[0].rearrange("p j r -> p (j r)").bitcast(I32)
        list_cols = SLOT_CHUNK // LIST_ROWS

        def look_up(t, c):
            entries = slice(c * list_cols, (c + 1) * list_cols)
            gate = keep.tile([P, SLOT_CHUNK], F32, name=f"gate{t}_{c}")
            nc.scalar.activation(out=gate[:], in_=g_rows[t][:].indirect(gate_list[:, entries]), func=SIGMOID)
            nc.vector.tensor_tensor(y[c][:, t, :], v_rows[t][:].indirect(value_list[:, entries]), gate[:], MULT)

        def store_rows(c, t0, t1):
            cols = slice(c * SLOT_CHUNK, (c + 1) * SLOT_CHUNK)
            nc.sync.dma_start(out=y_rows[:, t0:t1, cols], in_=y[c][:, t0:t1, :])

        def quantise_result(c, engine_copy):
            cols = slice(c * SLOT_CHUNK, (c + 1) * SLOT_CHUNK)
            grouped = keep.tile([P, SLOT_CHUNK * PACK], BF16, name=f"y_grouped{c}", align_bytes=64)
            engine_copy(
                out=grouped[:].rearrange("p (a i t) -> p a t i", i=4, t=PACK),
                in_=y[c][:].rearrange("p t (a i) -> p a t i", i=4),
            )
            codes = keep.tile([P, SLOT_CHUNK], U32, name=f"y_codes{c}", align_bytes=64)
            nc.vector.quantize_mx(out=codes[:].bitcast(FP8X4), scales=y_scales[:, cols], in_=grouped[:])
            nc.sync.dma_start(out=y_words[:, cols], in_=codes[:].bitcast(I32))

        late_gate(0, on_scalar)
        late_gate(1, on_vector)
        values(0, on_vector)
        look_up(0, 0)
        values(1, on_vector)
        look_up(1, 0)
        store_rows(0, 0, 2)
        late_gate(2, on_scalar)
        values(2, on_vector)
        look_up(2, 0)
        late_gate(3, on_scalar)
        values(3, on_scalar)
        look_up(3, 0)
        store_rows(0, 2, 4)
        for t in range(PACK):
            look_up(t, 1)
            if t % 2 == 1:
                store_rows(1, t - 1, t + 1)
        quantise_result(0, on_scalar)
        quantise_result(1, on_vector)

        scale_words = y_scales[:].bitcast(I32)
        for q in range(QUADS):
            queue = nc.scalar if q % 2 == 0 else nc.sync
            queue.dma_start(
                out=out_2[0, 4 * q : 4 * q + 4, :].bitcast(I32),
                in_=scale_words[32 * q : 32 * q + 4, :],
            )
